import numpy as np
import ml_dtypes


def mxq(x, axis, fmt="e4m3"):
    dtype, down = {"e4m3": (ml_dtypes.float8_e4m3fn, 7), "e5m2": (ml_dtypes.float8_e5m2, 14)}[fmt]
    v = np.moveaxis(np.asarray(x, np.float32).astype(ml_dtypes.bfloat16).astype(np.float64), axis, -1)
    blocks = v.reshape(v.shape[:-1] + (-1, 32))
    amax = np.abs(blocks).max(-1, keepdims=True)
    byte = np.maximum(np.where(amax > 0, np.frexp(amax)[1] - 1 + 127, 0) - down, 1)
    scale = np.exp2(byte - 127.0)
    codes = (blocks / scale).astype(np.float32).astype(dtype).astype(np.float64)
    return np.moveaxis((codes * scale).reshape(v.shape), -1, axis)


WIDE = False


def mx_kscale(k):
    if not WIDE:
        return np.ones(k)
    levels = np.array([10, -10, 5, -5, 0])
    if k % 512:
        return np.exp2(np.random.permutation(np.resize(levels, k // 32))).repeat(32)
    a = np.empty((k // 512, 16))
    for p in range(k // 512):
        a[p, :8] = np.random.permutation(np.resize(levels, 8))
        for g in range(8):
            far = levels[np.abs(levels - a[p, g]) >= 10]
            a[p, g + 8] = far[np.random.randint(len(far))]
    return np.exp2(a.ravel()).repeat(32)


def f64(x):
    return np.asarray(x).astype(np.float64)


def striped(idx):
    return np.tile(idx.reshape(-1, 16).T, (8, 1)).astype(np.uint16)


def unstriped(offs):
    return offs[:16].T.reshape(-1).astype(np.int64)


E2M1 = np.array([0.0, 0.5, 1.0, 1.5, 2.0, 3.0, 4.0, 6.0, -0.0, -0.5, -1.0, -1.5, -2.0, -3.0, -4.0, -6.0])


def pack_weight(w, fmt):
    k, n = w.shape
    w = f64(np.asarray(w, np.float32).astype(ml_dtypes.bfloat16)).reshape(k // 32, 32, n)
    amax = np.abs(w).max(1)
    if fmt == "e4m3":
        byte = np.frexp(amax)[1] - 1 + 127 - 7
    else:
        mant, ex = np.frexp(amax / 6.0)
        byte = np.where(mant > 0.5, ex, ex - 1) + 127
    byte = np.clip(np.where(amax > 0, byte, 1), 1, 254)
    scaled = (w * np.exp2(127.0 - byte)[:, None, :]).reshape(k, n).astype(np.float32)
    by_word = np.ascontiguousarray(scaled.reshape(k // 512, 128, 4, n).transpose(0, 1, 3, 2))
    if fmt == "e4m3":
        words = by_word.astype(ml_dtypes.float8_e4m3fn).view(np.uint8)
    else:
        c = by_word.astype(ml_dtypes.float4_e2m1fn).view(np.uint8) & 0xF
        words = (c[..., 0::2] | (c[..., 1::2] << 4)).reshape(k // 512, 128, 2 * n)
    return np.ascontiguousarray(words), np.ascontiguousarray(byte.astype(np.uint8).reshape(k // 512, 16, n))


def unpack_weight(words, scales, fmt):
    g, _, n = scales.shape
    words = np.ascontiguousarray(words).reshape(g, 128, n, -1)
    if fmt == "e4m3":
        vals = words.view(ml_dtypes.float8_e4m3fn).astype(np.float64)
    else:
        nib = np.empty((g, 128, n, 4), np.uint8)
        nib[..., 0::2] = words & 0xF
        nib[..., 1::2] = words >> 4
        vals = E2M1[nib]
    vals = vals * np.repeat(np.exp2(scales.astype(np.float64) - 127.0), 8, axis=1)[..., None]
    return vals.transpose(0, 1, 3, 2).reshape(g * 512, n)


def gelu(v):
    return 0.5 * v * (1.0 + np.tanh(np.sqrt(2.0 / np.pi) * (v + 0.044715 * v**3)))


def bf(x):
    return np.asarray(x, np.float32).astype(ml_dtypes.bfloat16)


def planes(Y):
    n, m = Y.shape
    b = f64(bf(Y)).reshape(n // 32, 32, m)
    amax = np.abs(b).max(1)
    byte = np.clip(np.where(amax > 0, np.frexp(amax)[1] - 1 + 127 - 7, 1), 1, 254)
    codes = (b * np.exp2(127.0 - byte)[:, None, :]).reshape(n, m).astype(np.float32).astype(ml_dtypes.float8_e4m3fn).view(np.uint8)
    words = codes.reshape(n // 512, 128, 4, m).transpose(0, 1, 3, 2)
    return np.ascontiguousarray(words), np.ascontiguousarray(byte.astype(np.uint8).reshape(n // 512, 16, m))


T, S, K, H, N, P = 4096, 1024, 1536, 1024, 512, 512


def setup_inputs():
    n = np.random.standard_normal
    s = mx_kscale(K)[:, None]
    u = mx_kscale(H)[:, None]
    size = np.exp(0.8 * n(N))
    d = {}
    d["tab_words"], d["tab_scales"] = pack_weight(n((K, T)) * s, "e2m1")
    d["offs"] = striped(np.random.permutation(T)[:S])
    d["pos1"] = striped(np.random.permutation(S)[:P])
    d["pos2"] = striped(np.random.permutation(S)[:P])
    d["w1"] = (n((K, H)) / K ** 0.5 / s).astype(np.float32)
    d["kap"] = (np.exp(0.3 * n(H)) * u[:, 0]).astype(np.float32)
    d["w4_words"], d["w4_scales"] = pack_weight(1.5 * n((H, N)) / H ** 0.5 / u * size, "e2m1")
    d["base"] = (0.7 * n((N, P)) * size[:, None]).astype(np.float32)
    return d


def reference(tab_words, tab_scales, offs, pos1, pos2, w1, kap, w4_words, w4_scales, base):
    v = unpack_weight(tab_words, tab_scales, "e2m1")[:, unstriped(offs)]
    logc = mxq(f64(w1), 0, "e4m3").T @ v
    h = f64(kap)[:, None] * np.exp(logc)
    res1 = 1.0 / h[:, unstriped(pos1)]
    res2 = 1.0 / h[:, unstriped(pos2)]
    z = 1.0 / (res1 + res2)
    w4 = unpack_weight(w4_words, w4_scales, "e2m1")
    y = (w4.T @ mxq(z, 0, "e4m3")) - f64(base)
    words, scales = planes(y)
    return y, words, scales

@@ -1,0 +1,268 @@
+from contextlib import ExitStack
+
+import concourse.mybir as mybir
+
+T, S, K, H, N, J = 4096, 1024, 1536, 1024, 512, 512
+FLOPS = 2 * K * H * S + 2 * H * N * J
+
+F32 = mybir.dt.float32
+BF16 = mybir.dt.bfloat16
+I32 = mybir.dt.int32
+U32 = mybir.dt.uint32
+U16 = mybir.dt.uint16
+U8 = mybir.dt.uint8
+FP8X4 = mybir.dt.float8_e4m3fn_x4
+FP4X4 = mybir.dt.float4_e2m1fn_x4
+ACT = mybir.ActivationFunctionType
+ALU = mybir.AluOpType
+
+P = 128
+PACK = 4
+PASS = P * PACK
+K_PASSES = K // PASS
+R_PASSES = H // PASS
+BANK = 512
+HALF = J // 2
+QUARTER = J // 4
+VECTOR_WORDS = 80
+
+
+def tile_list_doublet_series_flow_kernel(
+    tc, tab_words, tab_scales, offs, pos1, pos2, w1, kap, w4_words, w4_scales, base, out_0, out_1, out_2
+):
+    nc = tc.nc
+    with ExitStack() as ctx:
+        sb = ctx.enter_context(tc.tile_pool(name="sb", bufs=1))
+        ring = ctx.enter_context(tc.tile_pool(name="ring", bufs=4))
+        ps = ctx.enter_context(tc.psum_pool(name="ps", bufs=1))
+
+        def tile(name, shape, dtype):
+            return sb.tile(shape, dtype, name=name, align_bytes=64)
+
+        def load_buffer(name, shape, dtype):
+            return ring.tile(shape, dtype, name=name, tag="load", align_bytes=64)
+
+        banks = [ps.tile([P, BANK], F32, name="bank%d" % b) for b in range(8)]
+
+        offs_t = tile("offs_t", [P, S // 16], U16)
+        pos1_t = tile("pos1_t", [P, J // 16], U16)
+        pos2_t = tile("pos2_t", [P, J // 16], U16)
+        table = {}
+        table_sc = tile("table_sc", [P, T], U8)
+        v_words = [tile("v_words%d" % a, [P, S], U16) for a in range(K_PASSES)]
+        picked_sc = tile("picked_sc", [P, S], U8)
+        v_sc = tile("v_sc", [P, K_PASSES * S], U8)
+        pieces = [(g, a) for g in range(R_PASSES) for a in range(K_PASSES)]
+        w1_raw = {}
+        w1_bf = {ga: tile("w1_bf%d%d" % ga, [P, PACK * PASS], BF16) for ga in pieces[:-1]}
+        w1_bf[1, 2] = w1_bf[1, 0]
+        w1_words = {ga: tile("w1_words%d%d" % ga, [P, PASS], U32) for ga in pieces}
+        w1_sc = {ga: tile("w1_sc%d%d" % ga, [P, PASS], U8) for ga in pieces}
+        w4_raw = tile("w4_raw", [P, R_PASSES * N], U16)
+        w4_sc_raw = tile("w4_sc_raw", [P, R_PASSES * N], U8)
+        w4_dealt = tile("w4_dealt", [P, R_PASSES * N], U16)
+        w4_sc = tile("w4_sc", [P, R_PASSES * N], U8)
+        kap_t = tile("kap_t", [P, R_PASSES * PACK], F32)
+        inv_kap = tile("inv_kap", [P, R_PASSES * PACK], F32)
+        factor = tile("factor", [P, R_PASSES * PACK], F32)
+        res = [tile("res%d" % s, [P, S], F32) for s in range(R_PASSES * PACK)]
+        picked = [tile("picked%d" % i, [P, HALF], F32) for i in range(2)]
+        units = [(0, t, h) for t in range(PACK) for h in range(2)] + [(1, t, h) for h in range(2) for t in range(PACK)]
+        total = {u: tile("total%d%d%d" % u, [P, HALF], F32) for u in units}
+        root = {(g, h): tile("root%d%d" % (g, h), [P, PACK, HALF], F32) for g in range(R_PASSES) for h in range(2)}
+        z_bf = {(g, h): tile("z_bf%d%d" % (g, h), [P, HALF * PACK], BF16) for g in range(R_PASSES) for h in range(2)}
+        z_words = {(g, h): tile("z_words%d%d" % (g, h), [P, HALF], U32) for g in range(R_PASSES) for h in range(2)}
+        z_sc = {(g, h): tile("z_sc%d%d" % (g, h), [P, HALF], U8) for g in range(R_PASSES) for h in range(2)}
+        y = [tile("y%d" % h, [P, PACK, HALF], F32) for h in range(2)]
+        y_bf = [tile("y_bf%d" % h, [P, HALF * PACK], BF16) for h in range(2)]
+        y_words = tile("y_words", [P, J], U32)
+        y_sc = tile("y_sc", [P, J], U8)
+
+        nc.vector.memset(table_sc[:].bitcast(I32)[:, :704], 0)
+        nc.gpsimd.memset(table_sc[:].bitcast(I32)[:, 704:], 0)
+        nc.vector.memset(w4_sc_raw[:].bitcast(I32), 0)
+        nc.vector.memset(v_sc[:].bitcast(I32), 0)
+        nc.vector.memset(factor[:], -1.0)
+
+        def load_w1(g, a):
+            rows = w1[a * PASS : (a + 1) * PASS, g * PASS : (g + 1) * PASS]
+            w1_raw[g, a] = load_buffer("w1_raw%d%d" % (g, a), [P, PACK, PASS], F32)
+            nc.sync.dma_start(w1_raw[g, a][:], rows.rearrange("(p j) c -> p j c", j=PACK))
+
+        def load_table(a):
+            table[a] = load_buffer("table%d" % a, [P, T], U16)
+            nc.sync.dma_start(table[a][:].bitcast(I32), tab_words[a].bitcast(I32))
+
+        load_table(0)
+        nc.sync.dma_start(table_sc[0:96:2, :].bitcast(I32), tab_scales.bitcast(I32).rearrange("a q t -> q a t"))
+        nc.sync.dma_start(offs_t[:], offs)
+        nc.sync.dma_start(pos1_t[:], pos1)
+        nc.vector.tensor_copy(picked_sc[:], table_sc[:].indirect(offs_t[:]))
+        load_w1(0, 0)
+        load_table(1)
+        load_w1(0, 1)
+        nc.sync.dma_start(
+            w4_raw[:].bitcast(I32).rearrange("p (a c) -> p a c", a=R_PASSES),
+            w4_words.bitcast(I32).rearrange("a p c -> p a c"),
+        )
+        for q in range(4):
+            nc.sync.dma_start(
+                v_sc[32 * q : 32 * q + 4, :].bitcast(I32), picked_sc[24 * q : 24 * q + 24 : 2, :].bitcast(I32)
+            )
+        load_table(2)
+        load_w1(0, 2)
+        for q in range(4):
+            nc.sync.dma_start(
+                w4_sc_raw[32 * q : 32 * q + 4, :].bitcast(I32).rearrange("r (a c) -> r a c", a=R_PASSES),
+                w4_scales[:, 4 * q : 4 * q + 4, :].bitcast(I32).rearrange("a r c -> r a c"),
+            )
+        nc.sync.dma_start(pos2_t[:], pos2)
+        nc.sync.dma_start(
+            kap_t[:].rearrange("p (g t) -> p g t", g=R_PASSES),
+            kap.rearrange("(g p t) -> p g t", g=R_PASSES, t=PACK),
+        )
+        for a in range(K_PASSES):
+            load_w1(1, a)
+        base_t = load_buffer("base_t", [P, PACK, J], F32)
+        nc.sync.dma_start(base_t[:], base.rearrange("(p t) j -> p t j", t=PACK))
+
+        def quantise_w1(g, a, vector_words):
+            src = w1_raw[g, a][:].rearrange("p j (m t) -> p m j t", t=PACK)
+            dst = w1_bf[g, a][:].rearrange("p (t m j) -> p m j t", t=PACK, j=PACK)
+            if vector_words:
+                nc.vector.tensor_copy(dst[:, :vector_words], src[:, :vector_words])
+            nc.scalar.copy(dst[:, vector_words:], src[:, vector_words:])
+            nc.vector.quantize_mx(w1_words[g, a][:].bitcast(FP8X4), w1_sc[g, a][:], w1_bf[g, a][:])
+
+        def first_product(g, a, slices=range(PACK)):
+            for t in slices:
+                cols = slice(t * P, (t + 1) * P)
+                for h in range(2):
+                    m = slice(h * BANK, (h + 1) * BANK)
+                    nc.tensor.matmul_mx(
+                        banks[2 * t + h][:],
+                        lhsT=w1_words[g, a][:, cols].bitcast(FP8X4),
+                        lhsT_scale=w1_sc[g, a][:, cols],
+                        rhs=v_words[a][:, m].bitcast(FP4X4),
+                        rhs_scale=v_sc[:, a * S + h * BANK : a * S + (h + 1) * BANK],
+                        start=(a == 0),
+                        stop=(a == K_PASSES - 1),
+                    )
+
+        def resistances(g, slices=range(PACK)):
+            for t in slices:
+                s = g * PACK + t
+                for h in range(2):
+                    nc.scalar.activation(
+                        res[s][:, h * BANK : (h + 1) * BANK], banks[2 * t + h][:], ACT.Exp, scale=factor[:, s : s + 1]
+                    )
+
+        def entries(h):
+            return slice(h * HALF // 16, (h + 1) * HALF // 16)
+
+        def landing(i):
+            if i in (0, 4, 6):
+                return w1_bf[1, 0][:].bitcast(F32)[:, :HALF]
+            if i == 1:
+                return w1_bf[1, 0][:].bitcast(F32)[:, HALF : 2 * HALF]
+            if i == 2:
+                return w1_bf[1, 1][:].bitcast(F32)[:, :HALF]
+            return picked[i % 2][:]
+
+        def pick_first(i):
+            g, t, h = units[i]
+            nc.vector.tensor_copy(landing(i), res[g * PACK + t][:].indirect(pos1_t[:, entries(h)]))
+
+        def pick_second(i):
+            g, t, h = units[i]
+            nc.vector.tensor_tensor(
+                total[g, t, h][:], res[g * PACK + t][:].indirect(pos2_t[:, entries(h)]), landing(i), ALU.add
+            )
+
+        def pick(first, last):
+            for i in range(first, last, 2):
+                pick_first(i)
+                pick_first(i + 1)
+                pick_second(i)
+                pick_second(i + 1)
+
+        def make_z(g, h):
+            for t in range(PACK):
+                s = g * PACK + t
+                nc.scalar.activation(
+                    root[g, h][:, t, :], total[g, t, h][:], ACT.Abs_reciprocal_sqrt, scale=factor[:, s : s + 1]
+                )
+            nc.scalar.activation(
+                z_bf[g, h][:].rearrange("p (c i t) -> p c t i", i=4, t=PACK),
+                root[g, h][:].rearrange("p t (c i) -> p c t i", i=4),
+                ACT.Square,
+            )
+            nc.vector.quantize_mx(z_words[g, h][:].bitcast(FP8X4), z_sc[g, h][:], z_bf[g, h][:])
+
+        def finish(h):
+            for quarter in range(2):
+                local = slice(quarter * QUARTER, (quarter + 1) * QUARTER)
+                j0 = h * HALF + quarter * QUARTER
+                bank = banks[2 * (2 * h + quarter)][:].rearrange("p (t j) -> p t j", t=PACK)
+                for t in range(PACK):
+                    for g in range(R_PASSES):
+                        cols = slice(g * N + t * P, g * N + (t + 1) * P)
+                        nc.tensor.matmul_mx(
+                            bank[:, t, :],
+                            lhsT=w4_dealt[:, cols].bitcast(FP4X4),
+                            lhsT_scale=w4_sc[:, cols],
+                            rhs=z_words[g, h][:, local].bitcast(FP8X4),
+                            rhs_scale=z_sc[g, h][:, local],
+                            start=(g == 0),
+                            stop=(g == R_PASSES - 1),
+                        )
+                nc.vector.tensor_tensor(y[h][:, :, local], bank, base_t[:, :, j0 : j0 + QUARTER], ALU.subtract)
+            js = slice(h * HALF, (h + 1) * HALF)
+            nc.sync.dma_start(out_0.rearrange("(p t) j -> p t j", t=PACK)[:, :, js], y[h][:])
+            nc.vector.tensor_copy(
+                y_bf[h][:].rearrange("p (c i t) -> p c t i", i=4, t=PACK),
+                y[h][:].rearrange("p t (c i) -> p c t i", i=4),
+            )
+            nc.vector.quantize_mx(y_words[:, js].bitcast(FP8X4), y_sc[:, js], y_bf[h][:])
+            nc.sync.dma_start(
+                out_1[0].rearrange("p m t -> p (m t)").bitcast(I32)[:, js], y_words[:, js].bitcast(I32)
+            )
+
+        for a in range(K_PASSES):
+            nc.vector.tensor_copy(v_words[a][:], table[a][:].indirect(offs_t[:]))
+            quantise_w1(0, a, VECTOR_WORDS if a == K_PASSES - 1 else 0)
+            first_product(0, a)
+        nc.vector.reciprocal(inv_kap[:], kap_t[:])
+        nc.vector.tensor_copy(
+            w4_dealt[:].rearrange("p (a t q) -> p a q t", a=R_PASSES, t=PACK),
+            w4_raw[:].rearrange("p (a q t) -> p a q t", a=R_PASSES, t=PACK),
+        )
+        nc.vector.tensor_copy(
+            w4_sc[:].rearrange("p (a t q) -> p a q t", a=R_PASSES, t=PACK),
+            w4_sc_raw[:].rearrange("p (a q t) -> p a q t", a=R_PASSES, t=PACK),
+        )
+        resistances(0, range(3))
+        pick(0, 4)
+        quantise_w1(1, 0, 0)
+        first_product(1, 0, range(3))
+        pick(4, 6)
+        quantise_w1(1, 1, 0)
+        resistances(0, [3])
+        first_product(1, 0, [3])
+        quantise_w1(1, 2, VECTOR_WORDS)
+        pick(6, 8)
+        for t in range(PACK):
+            first_product(1, 1, [t])
+            first_product(1, 2, [t])
+        resistances(1)
+        nc.scalar.copy(factor[:], inv_kap[:])
+        pick(8, len(units))
+        make_z(0, 0)
+        make_z(0, 1)
+        make_z(1, 0)
+        make_z(1, 1)
+        finish(0)
+        finish(1)
+        for q in range(4):
+            engine = nc.sync if q % 2 == 0 else nc.scalar
+            engine.dma_start(out_2[0, 4 * q : 4 * q + 4, :].bitcast(I32), y_sc[32 * q : 32 * q + 4, :].bitcast(I32))

@@ -68,13 +68,13 @@ def tile_list_doublet_series_flow_kernel(
         res = [tile("res%d" % s, [P, S], F32) for s in range(R_PASSES * PACK)]
         picked = [tile("picked%d" % i, [P, HALF], F32) for i in range(2)]
         units = [(0, t, h) for t in range(PACK) for h in range(2)] + [(1, t, h) for h in range(2) for t in range(PACK)]
-        total = {u: tile("total%d%d%d" % u, [P, HALF], F32) for u in units}
-        root = {(g, h): tile("root%d%d" % (g, h), [P, PACK, HALF], F32) for g in range(R_PASSES) for h in range(2)}
-        z_bf = {(g, h): tile("z_bf%d%d" % (g, h), [P, HALF * PACK], BF16) for g in range(R_PASSES) for h in range(2)}
-        z_words = {(g, h): tile("z_words%d%d" % (g, h), [P, HALF], U32) for g in range(R_PASSES) for h in range(2)}
-        z_sc = {(g, h): tile("z_sc%d%d" % (g, h), [P, HALF], U8) for g in range(R_PASSES) for h in range(2)}
-        y = [tile("y%d" % h, [P, PACK, HALF], F32) for h in range(2)]
-        y_bf = [tile("y_bf%d" % h, [P, HALF * PACK], BF16) for h in range(2)]
+        total = [tile("total%d" % s, [P, J], F32) for s in range(R_PASSES * PACK)]
+        root = [tile("root%d" % g, [P, PACK, J], F32) for g in range(R_PASSES)]
+        z_bf = [tile("z_bf%d" % g, [P, J * PACK], BF16) for g in range(R_PASSES)]
+        z_words = [tile("z_words%d" % g, [P, J], U32) for g in range(R_PASSES)]
+        z_sc = [tile("z_sc%d" % g, [P, J], U8) for g in range(R_PASSES)]
+        y = tile("y", [P, PACK, J], F32)
+        y_bf = tile("y_bf", [P, J * PACK], BF16)
         y_words = tile("y_words", [P, J], U32)
         y_sc = tile("y_sc", [P, J], U8)
 
@@ -84,10 +84,14 @@ def tile_list_doublet_series_flow_kernel(
         nc.vector.memset(v_sc[:].bitcast(I32), 0)
         nc.vector.memset(factor[:], -1.0)
 
-        def load_w1(g, a):
+        def load_w1(g, a, parts=1):
             rows = w1[a * PASS : (a + 1) * PASS, g * PASS : (g + 1) * PASS]
-            w1_raw[g, a] = load_buffer("w1_raw%d%d" % (g, a), [P, PACK, PASS], F32)
-            nc.sync.dma_start(w1_raw[g, a][:], rows.rearrange("(p j) c -> p j c", j=PACK))
+            width = PASS // parts
+            w1_raw[g, a] = load_buffer("w1_raw%d%d" % (g, a), [P, parts, PACK, width], F32)
+            for u in range(parts):
+                nc.sync.dma_start(
+                    w1_raw[g, a][:, u], rows[:, u * width : (u + 1) * width].rearrange("(p j) c -> p j c", j=PACK)
+                )
 
         def load_table(a):
             table[a] = load_buffer("table%d" % a, [P, T], U16)
@@ -110,7 +114,7 @@ def tile_list_doublet_series_flow_kernel(
                 v_sc[32 * q : 32 * q + 4, :].bitcast(I32), picked_sc[24 * q : 24 * q + 24 : 2, :].bitcast(I32)
             )
         load_table(2)
-        load_w1(0, 2)
+        load_w1(0, 2, parts=2)
         for q in range(4):
             nc.sync.dma_start(
                 w4_sc_raw[32 * q : 32 * q + 4, :].bitcast(I32).rearrange("r (a c) -> r a c", a=R_PASSES),
@@ -127,12 +131,21 @@ def tile_list_doublet_series_flow_kernel(
         nc.sync.dma_start(base_t[:], base.rearrange("(p t) j -> p t j", t=PACK))
 
         def quantise_w1(g, a, vector_words):
-            src = w1_raw[g, a][:].rearrange("p j (m t) -> p m j t", t=PACK)
             dst = w1_bf[g, a][:].rearrange("p (t m j) -> p m j t", t=PACK, j=PACK)
+            split = P - vector_words
+            if (g, a) == (0, K_PASSES - 1):
+                early, late = [w1_raw[g, a][:, u].rearrange("p j (m t) -> p m j t", t=PACK) for u in range(2)]
+            else:
+                src = w1_raw[g, a][:, 0].rearrange("p j (m t) -> p m j t", t=PACK)
+                early, late = src[:, :split], src[:, split:]
+            nc.scalar.copy(dst[:, :split], early)
             if vector_words:
-                nc.vector.tensor_copy(dst[:, :vector_words], src[:, :vector_words])
-            nc.scalar.copy(dst[:, vector_words:], src[:, vector_words:])
-            nc.vector.quantize_mx(w1_words[g, a][:].bitcast(FP8X4), w1_sc[g, a][:], w1_bf[g, a][:])
+                nc.vector.tensor_copy(dst[:, split:], late)
+            cuts = [0, P, 2 * P, PASS] if a == K_PASSES - 1 else [0, PASS]
+            for c0, c1 in zip(cuts, cuts[1:]):
+                nc.vector.quantize_mx(
+                    w1_words[g, a][:, c0:c1].bitcast(FP8X4), w1_sc[g, a][:, c0:c1], w1_bf[g, a][:, PACK * c0 : PACK * c1]
+                )
 
         def first_product(g, a, slices=range(PACK)):
             for t in slices:
@@ -161,12 +174,16 @@ def tile_list_doublet_series_flow_kernel(
             return slice(h * HALF // 16, (h + 1) * HALF // 16)
 
         def landing(i):
-            if i in (0, 4, 6):
+            if i in (0, 4):
                 return w1_bf[1, 0][:].bitcast(F32)[:, :HALF]
-            if i == 1:
-                return w1_bf[1, 0][:].bitcast(F32)[:, HALF : 2 * HALF]
             if i == 2:
                 return w1_bf[1, 1][:].bitcast(F32)[:, :HALF]
+            if i == 12:
+                return z_bf[0][:].bitcast(F32)[:, :HALF]
+            if i == 14:
+                return z_bf[0][:].bitcast(F32)[:, J : J + HALF]
+            if i == 15:
+                return z_bf[1][:].bitcast(F32)[:, :HALF]
             return picked[i % 2][:]
 
         def pick_first(i):
@@ -176,7 +193,7 @@ def tile_list_doublet_series_flow_kernel(
         def pick_second(i):
             g, t, h = units[i]
             nc.vector.tensor_tensor(
-                total[g, t, h][:], res[g * PACK + t][:].indirect(pos2_t[:, entries(h)]), landing(i), ALU.add
+                total[g * PACK + t][:, h * HALF : (h + 1) * HALF], res[g * PACK + t][:].indirect(pos2_t[:, entries(h)]), landing(i), ALU.add
             )
 
         def pick(first, last):
@@ -186,83 +203,100 @@ def tile_list_doublet_series_flow_kernel(
                 pick_second(i)
                 pick_second(i + 1)
 
-        def make_z(g, h):
+        def roots(g, js):
             for t in range(PACK):
                 s = g * PACK + t
                 nc.scalar.activation(
-                    root[g, h][:, t, :], total[g, t, h][:], ACT.Abs_reciprocal_sqrt, scale=factor[:, s : s + 1]
+                    root[g][:, t, js], total[s][:, js], ACT.Abs_reciprocal_sqrt, scale=factor[:, s : s + 1]
                 )
+
+        def interleaved(bf_tile, js):
+            return bf_tile[:, PACK * js.start : PACK * js.stop]
+
+        def make_z(g, js):
             nc.scalar.activation(
-                z_bf[g, h][:].rearrange("p (c i t) -> p c t i", i=4, t=PACK),
-                root[g, h][:].rearrange("p t (c i) -> p c t i", i=4),
+                interleaved(z_bf[g], js).rearrange("p (c i t) -> p c t i", i=4, t=PACK),
+                root[g][:, :, js].rearrange("p t (c i) -> p c t i", i=4),
                 ACT.Square,
             )
-            nc.vector.quantize_mx(z_words[g, h][:].bitcast(FP8X4), z_sc[g, h][:], z_bf[g, h][:])
+            nc.vector.quantize_mx(z_words[g][:, js].bitcast(FP8X4), z_sc[g][:, js], interleaved(z_bf[g], js))
 
-        def finish(h):
-            for quarter in range(2):
-                local = slice(quarter * QUARTER, (quarter + 1) * QUARTER)
-                j0 = h * HALF + quarter * QUARTER
-                bank = banks[2 * (2 * h + quarter)][:].rearrange("p (t j) -> p t j", t=PACK)
-                for t in range(PACK):
-                    for g in range(R_PASSES):
-                        cols = slice(g * N + t * P, g * N + (t + 1) * P)
-                        nc.tensor.matmul_mx(
-                            bank[:, t, :],
-                            lhsT=w4_dealt[:, cols].bitcast(FP4X4),
-                            lhsT_scale=w4_sc[:, cols],
-                            rhs=z_words[g, h][:, local].bitcast(FP8X4),
-                            rhs_scale=z_sc[g, h][:, local],
-                            start=(g == 0),
-                            stop=(g == R_PASSES - 1),
-                        )
-                nc.vector.tensor_tensor(y[h][:, :, local], bank, base_t[:, :, j0 : j0 + QUARTER], ALU.subtract)
-            js = slice(h * HALF, (h + 1) * HALF)
-            nc.sync.dma_start(out_0.rearrange("(p t) j -> p t j", t=PACK)[:, :, js], y[h][:])
-            nc.vector.tensor_copy(
-                y_bf[h][:].rearrange("p (c i t) -> p c t i", i=4, t=PACK),
-                y[h][:].rearrange("p t (c i) -> p c t i", i=4),
+        def sums(quarter):
+            return banks[2 * quarter][:].rearrange("p (t j) -> p t j", t=PACK)
+
+        def second_product(g, quarter):
+            js = slice(quarter * QUARTER, (quarter + 1) * QUARTER)
+            for t in range(PACK):
+                cols = slice(g * N + t * P, g * N + (t + 1) * P)
+                nc.tensor.matmul_mx(
+                    sums(quarter)[:, t, :],
+                    lhsT=w4_dealt[:, cols].bitcast(FP4X4),
+                    lhsT_scale=w4_sc[:, cols],
+                    rhs=z_words[g][:, js].bitcast(FP8X4),
+                    rhs_scale=z_sc[g][:, js],
+                    start=(g == 0 and t == 0),
+                    stop=(g == R_PASSES - 1 and t == PACK - 1),
+                )
+
+        def finish(js, round_y):
+            for quarter in range(js.start // QUARTER, js.stop // QUARTER):
+                second_product(1, quarter)
+                part = slice(quarter * QUARTER, (quarter + 1) * QUARTER)
+                nc.vector.tensor_tensor(y[:, :, part], sums(quarter), base_t[:, :, part], ALU.subtract)
+            nc.sync.dma_start(out_0.rearrange("(p t) j -> p t j", t=PACK)[:, :, js], y[:, :, js])
+            round_y(
+                interleaved(y_bf, js).rearrange("p (c i t) -> p c t i", i=4, t=PACK),
+                y[:, :, js].rearrange("p t (c i) -> p c t i", i=4),
             )
-            nc.vector.quantize_mx(y_words[:, js].bitcast(FP8X4), y_sc[:, js], y_bf[h][:])
+            nc.vector.quantize_mx(y_words[:, js].bitcast(FP8X4), y_sc[:, js], interleaved(y_bf, js))
             nc.sync.dma_start(
                 out_1[0].rearrange("p m t -> p (m t)").bitcast(I32)[:, js], y_words[:, js].bitcast(I32)
             )
 
         for a in range(K_PASSES):
             nc.vector.tensor_copy(v_words[a][:], table[a][:].indirect(offs_t[:]))
-            quantise_w1(0, a, VECTOR_WORDS if a == K_PASSES - 1 else 0)
+            quantise_w1(0, a, P // 2 if a == K_PASSES - 1 else 0)
             first_product(0, a)
         nc.vector.reciprocal(inv_kap[:], kap_t[:])
         nc.vector.tensor_copy(
-            w4_dealt[:].rearrange("p (a t q) -> p a q t", a=R_PASSES, t=PACK),
-            w4_raw[:].rearrange("p (a q t) -> p a q t", a=R_PASSES, t=PACK),
+            w4_dealt[:].rearrange("p (a t q) -> p a t q", a=R_PASSES, t=PACK),
+            w4_raw[:].rearrange("p (a q t) -> p a t q", a=R_PASSES, t=PACK),
         )
         nc.vector.tensor_copy(
-            w4_sc[:].rearrange("p (a t q) -> p a q t", a=R_PASSES, t=PACK),
-            w4_sc_raw[:].rearrange("p (a q t) -> p a q t", a=R_PASSES, t=PACK),
+            w4_sc[:].rearrange("p (a t q) -> p a t q", a=R_PASSES, t=PACK),
+            w4_sc_raw[:].rearrange("p (a q t) -> p a t q", a=R_PASSES, t=PACK),
         )
         resistances(0, range(3))
         pick(0, 4)
         quantise_w1(1, 0, 0)
         first_product(1, 0, range(3))
-        pick(4, 6)
-        quantise_w1(1, 1, 0)
+        quantise_w1(1, 1, 32)
+        quantise_w1(1, 2, VECTOR_WORDS)
         resistances(0, [3])
         first_product(1, 0, [3])
-        quantise_w1(1, 2, VECTOR_WORDS)
-        pick(6, 8)
+        pick(4, 8)
         for t in range(PACK):
             first_product(1, 1, [t])
             first_product(1, 2, [t])
         resistances(1)
         nc.scalar.copy(factor[:], inv_kap[:])
-        pick(8, len(units))
-        make_z(0, 0)
-        make_z(0, 1)
-        make_z(1, 0)
-        make_z(1, 1)
-        finish(0)
-        finish(1)
+        pick(8, 12)
+        for h in range(2):
+            roots(0, slice(h * HALF, (h + 1) * HALF))
+            make_z(0, slice(h * HALF, (h + 1) * HALF))
+            second_product(0, 2 * h)
+            second_product(0, 2 * h + 1)
+            if h == 0:
+                pick(12, 14)
+        roots(1, slice(0, HALF))
+        make_z(1, slice(0, HALF))
+        pick(14, 16)
+        roots(1, slice(HALF, J))
+        make_z(1, slice(HALF, HALF + QUARTER))
+        make_z(1, slice(HALF + QUARTER, J))
+        finish(slice(0, HALF), nc.scalar.copy)
+        finish(slice(HALF, HALF + QUARTER), nc.scalar.copy)
+        finish(slice(HALF + QUARTER, J), nc.vector.tensor_copy)
         for q in range(4):
             engine = nc.sync if q % 2 == 0 else nc.scalar
             engine.dma_start(out_2[0, 4 * q : 4 * q + 4, :].bitcast(I32), y_sc[32 * q : 32 * q + 4, :].bitcast(I32))

@@ -24,7 +24,7 @@ R_PASSES = H // PASS
 BANK = 512
 HALF = J // 2
 QUARTER = J // 4
-VECTOR_WORDS = 80
+CHUNK = 256
 
 
 def tile_list_doublet_series_flow_kernel(
@@ -33,7 +33,7 @@ def tile_list_doublet_series_flow_kernel(
     nc = tc.nc
     with ExitStack() as ctx:
         sb = ctx.enter_context(tc.tile_pool(name="sb", bufs=1))
-        ring = ctx.enter_context(tc.tile_pool(name="ring", bufs=4))
+        ring = ctx.enter_context(tc.tile_pool(name="ring", bufs=5))
         ps = ctx.enter_context(tc.psum_pool(name="ps", bufs=1))
 
         def tile(name, shape, dtype):
@@ -52,12 +52,13 @@ def tile_list_doublet_series_flow_kernel(
         v_words = [tile("v_words%d" % a, [P, S], U16) for a in range(K_PASSES)]
         picked_sc = tile("picked_sc", [P, S], U8)
         v_sc = tile("v_sc", [P, K_PASSES * S], U8)
-        pieces = [(g, a) for g in range(R_PASSES) for a in range(K_PASSES)]
+        blocks = [(0, CHUNK), (CHUNK, CHUNK), (PASS, PASS)]
+        pieces = [(b, a) for b in range(len(blocks)) for a in range(K_PASSES)]
         w1_raw = {}
-        w1_bf = {ga: tile("w1_bf%d%d" % ga, [P, PACK * PASS], BF16) for ga in pieces[:-1]}
-        w1_bf[1, 2] = w1_bf[1, 0]
-        w1_words = {ga: tile("w1_words%d%d" % ga, [P, PASS], U32) for ga in pieces}
-        w1_sc = {ga: tile("w1_sc%d%d" % ga, [P, PASS], U8) for ga in pieces}
+        w1_words = {(b, a): tile("w1_words%d%d" % (b, a), [P, blocks[b][1]], U32) for b, a in pieces}
+        w1_sc = {(b, a): tile("w1_sc%d%d" % (b, a), [P, blocks[b][1]], U8) for b, a in pieces}
+        stage = [tile("stage%d" % i, [P, PACK * CHUNK], BF16) for i in range(3)]
+        wide_stage = tile("wide_stage", [P, PACK * PASS], BF16)
         w4_raw = tile("w4_raw", [P, R_PASSES * N], U16)
         w4_sc_raw = tile("w4_sc_raw", [P, R_PASSES * N], U8)
         w4_dealt = tile("w4_dealt", [P, R_PASSES * N], U16)
@@ -66,10 +67,20 @@ def tile_list_doublet_series_flow_kernel(
         inv_kap = tile("inv_kap", [P, R_PASSES * PACK], F32)
         factor = tile("factor", [P, R_PASSES * PACK], F32)
         res = [tile("res%d" % s, [P, S], F32) for s in range(R_PASSES * PACK)]
+        w1_bf = {
+            (0, 0): stage[0][:],
+            (0, 1): stage[1][:],
+            (0, 2): stage[2][:],
+            (1, 0): stage[0][:],
+            (1, 1): stage[2][:],
+            (1, 2): wide_stage[:, : PACK * CHUNK],
+            (2, 0): res[2][:].bitcast(BF16),
+            (2, 1): res[3][:].bitcast(BF16),
+            (2, 2): wide_stage[:],
+        }
         picked = [tile("picked%d" % i, [P, HALF], F32) for i in range(2)]
         units = [(0, t, h) for t in range(PACK) for h in range(2)] + [(1, t, h) for h in range(2) for t in range(PACK)]
         total = [tile("total%d" % s, [P, J], F32) for s in range(R_PASSES * PACK)]
-        root = [tile("root%d" % g, [P, PACK, J], F32) for g in range(R_PASSES)]
         z_bf = [tile("z_bf%d" % g, [P, J * PACK], BF16) for g in range(R_PASSES)]
         z_words = [tile("z_words%d" % g, [P, J], U32) for g in range(R_PASSES)]
         z_sc = [tile("z_sc%d" % g, [P, J], U8) for g in range(R_PASSES)]
@@ -84,14 +95,11 @@ def tile_list_doublet_series_flow_kernel(
         nc.vector.memset(v_sc[:].bitcast(I32), 0)
         nc.vector.memset(factor[:], -1.0)
 
-        def load_w1(g, a, parts=1):
-            rows = w1[a * PASS : (a + 1) * PASS, g * PASS : (g + 1) * PASS]
-            width = PASS // parts
-            w1_raw[g, a] = load_buffer("w1_raw%d%d" % (g, a), [P, parts, PACK, width], F32)
-            for u in range(parts):
-                nc.sync.dma_start(
-                    w1_raw[g, a][:, u], rows[:, u * width : (u + 1) * width].rearrange("(p j) c -> p j c", j=PACK)
-                )
+        def load_w1(b, a):
+            first, width = blocks[b]
+            rows = w1[a * PASS : (a + 1) * PASS, first : first + width]
+            w1_raw[b, a] = load_buffer("w1_raw%d%d" % (b, a), [P, PACK, width], F32)
+            nc.sync.dma_start(w1_raw[b, a][:], rows.rearrange("(p j) c -> p j c", j=PACK))
 
         def load_table(a):
             table[a] = load_buffer("table%d" % a, [P, T], U16)
@@ -105,79 +113,76 @@ def tile_list_doublet_series_flow_kernel(
         load_w1(0, 0)
         load_table(1)
         load_w1(0, 1)
+        load_table(2)
+        nc.sync.dma_start(pos2_t[:], pos2)
+        for q in range(4):
+            nc.sync.dma_start(
+                v_sc[32 * q : 32 * q + 4, :].bitcast(I32), picked_sc[24 * q : 24 * q + 24 : 2, :].bitcast(I32)
+            )
+        load_w1(0, 2)
+        for a in range(K_PASSES):
+            load_w1(1, a)
         nc.sync.dma_start(
             w4_raw[:].bitcast(I32).rearrange("p (a c) -> p a c", a=R_PASSES),
             w4_words.bitcast(I32).rearrange("a p c -> p a c"),
         )
         for q in range(4):
             nc.sync.dma_start(
-                v_sc[32 * q : 32 * q + 4, :].bitcast(I32), picked_sc[24 * q : 24 * q + 24 : 2, :].bitcast(I32)
-            )
-        load_table(2)
-        load_w1(0, 2, parts=2)
-        for q in range(4):
-            nc.sync.dma_start(
                 w4_sc_raw[32 * q : 32 * q + 4, :].bitcast(I32).rearrange("r (a c) -> r a c", a=R_PASSES),
                 w4_scales[:, 4 * q : 4 * q + 4, :].bitcast(I32).rearrange("a r c -> r a c"),
             )
-        nc.sync.dma_start(pos2_t[:], pos2)
         nc.sync.dma_start(
             kap_t[:].rearrange("p (g t) -> p g t", g=R_PASSES),
             kap.rearrange("(g p t) -> p g t", g=R_PASSES, t=PACK),
         )
         for a in range(K_PASSES):
-            load_w1(1, a)
+            load_w1(2, a)
         base_t = load_buffer("base_t", [P, PACK, J], F32)
         nc.sync.dma_start(base_t[:], base.rearrange("(p t) j -> p t j", t=PACK))
+        regrouped = load_buffer("regrouped", [P, PACK, J], F32)
+        root = [tile("root0", [P, PACK, J], F32), regrouped]
 
-        def quantise_w1(g, a, vector_words):
-            dst = w1_bf[g, a][:].rearrange("p (t m j) -> p m j t", t=PACK, j=PACK)
-            split = P - vector_words
-            if (g, a) == (0, K_PASSES - 1):
-                early, late = [w1_raw[g, a][:, u].rearrange("p j (m t) -> p m j t", t=PACK) for u in range(2)]
+        def quantise_w1(b, a, round_to_bf16):
+            raw, bf = w1_raw[b, a][:], w1_bf[b, a]
+            if b == 2:
+                round_to_bf16(
+                    bf.rearrange("p (t m j) -> p m j t", t=PACK, j=PACK), raw.rearrange("p j (m t) -> p m j t", t=PACK)
+                )
             else:
-                src = w1_raw[g, a][:, 0].rearrange("p j (m t) -> p m j t", t=PACK)
-                early, late = src[:, :split], src[:, split:]
-            nc.scalar.copy(dst[:, :split], early)
-            if vector_words:
-                nc.vector.tensor_copy(dst[:, split:], late)
-            cuts = [0, P, 2 * P, PASS] if a == K_PASSES - 1 else [0, PASS]
-            for c0, c1 in zip(cuts, cuts[1:]):
-                nc.vector.quantize_mx(
-                    w1_words[g, a][:, c0:c1].bitcast(FP8X4), w1_sc[g, a][:, c0:c1], w1_bf[g, a][:, PACK * c0 : PACK * c1]
+                round_to_bf16(
+                    bf.rearrange("p (c i j) -> p c j i", i=4, j=PACK), raw.rearrange("p j (c i) -> p c j i", i=4)
+                )
+            nc.vector.quantize_mx(w1_words[b, a][:].bitcast(FP8X4), w1_sc[b, a][:], bf)
+
+        def first_product(s, a):
+            b, u = (s // 2, s % 2) if s < PACK else (2, s - PACK)
+            cols = slice(u * P, (u + 1) * P)
+            for h in range(2):
+                nc.tensor.matmul_mx(
+                    banks[2 * (s % PACK) + h][:],
+                    lhsT=w1_words[b, a][:, cols].bitcast(FP8X4),
+                    lhsT_scale=w1_sc[b, a][:, cols],
+                    rhs=v_words[a][:, h * BANK : (h + 1) * BANK].bitcast(FP4X4),
+                    rhs_scale=v_sc[:, a * S + h * BANK : a * S + (h + 1) * BANK],
+                    start=(a == 0),
+                    stop=(a == K_PASSES - 1),
                 )
 
-        def first_product(g, a, slices=range(PACK)):
-            for t in slices:
-                cols = slice(t * P, (t + 1) * P)
-                for h in range(2):
-                    m = slice(h * BANK, (h + 1) * BANK)
-                    nc.tensor.matmul_mx(
-                        banks[2 * t + h][:],
-                        lhsT=w1_words[g, a][:, cols].bitcast(FP8X4),
-                        lhsT_scale=w1_sc[g, a][:, cols],
-                        rhs=v_words[a][:, m].bitcast(FP4X4),
-                        rhs_scale=v_sc[:, a * S + h * BANK : a * S + (h + 1) * BANK],
-                        start=(a == 0),
-                        stop=(a == K_PASSES - 1),
-                    )
-
-        def resistances(g, slices=range(PACK)):
-            for t in slices:
-                s = g * PACK + t
-                for h in range(2):
-                    nc.scalar.activation(
-                        res[s][:, h * BANK : (h + 1) * BANK], banks[2 * t + h][:], ACT.Exp, scale=factor[:, s : s + 1]
-                    )
+        def resistances(s):
+            for h in range(2):
+                nc.scalar.activation(
+                    res[s][:, h * BANK : (h + 1) * BANK],
+                    banks[2 * (s % PACK) + h][:],
+                    ACT.Exp,
+                    scale=factor[:, s : s + 1],
+                )
 
         def entries(h):
             return slice(h * HALF // 16, (h + 1) * HALF // 16)
 
         def landing(i):
-            if i in (0, 4):
-                return w1_bf[1, 0][:].bitcast(F32)[:, :HALF]
-            if i == 2:
-                return w1_bf[1, 1][:].bitcast(F32)[:, :HALF]
+            if i in (0, 2):
+                return wide_stage[:].bitcast(F32)[:, :HALF]
             if i == 12:
                 return z_bf[0][:].bitcast(F32)[:, :HALF]
             if i == 14:
@@ -195,6 +200,9 @@ def tile_list_doublet_series_flow_kernel(
             nc.vector.tensor_tensor(
                 total[g * PACK + t][:, h * HALF : (h + 1) * HALF], res[g * PACK + t][:].indirect(pos2_t[:, entries(h)]), landing(i), ALU.add
             )
+            if g == 0:
+                js = slice(h * HALF, (h + 1) * HALF)
+                nc.sync.dma_start(regrouped[32 * t : 32 * (t + 1), :, js], total[t][:, js])
 
         def pick(first, last):
             for i in range(first, last, 2):
@@ -206,8 +214,9 @@ def tile_list_doublet_series_flow_kernel(
         def roots(g, js):
             for t in range(PACK):
                 s = g * PACK + t
+                sums_of_pairs = regrouped[:, t, js] if g == 0 else total[s][:, js]
                 nc.scalar.activation(
-                    root[g][:, t, js], total[s][:, js], ACT.Abs_reciprocal_sqrt, scale=factor[:, s : s + 1]
+                    root[g][:, t, js], sums_of_pairs, ACT.Abs_reciprocal_sqrt, scale=factor[:, s : s + 1]
                 )
 
         def interleaved(bf_tile, js):
@@ -255,8 +264,13 @@ def tile_list_doublet_series_flow_kernel(
 
         for a in range(K_PASSES):
             nc.vector.tensor_copy(v_words[a][:], table[a][:].indirect(offs_t[:]))
-            quantise_w1(0, a, P // 2 if a == K_PASSES - 1 else 0)
+            quantise_w1(0, a, nc.scalar.copy)
             first_product(0, a)
+            first_product(1, a)
+        resistances(0)
+        resistances(1)
+        quantise_w1(1, 0, nc.scalar.copy)
+        quantise_w1(1, 1, nc.vector.tensor_copy)
         nc.vector.reciprocal(inv_kap[:], kap_t[:])
         nc.vector.tensor_copy(
             w4_dealt[:].rearrange("p (a t q) -> p a t q", a=R_PASSES, t=PACK),
@@ -266,19 +280,23 @@ def tile_list_doublet_series_flow_kernel(
             w4_sc[:].rearrange("p (a t q) -> p a t q", a=R_PASSES, t=PACK),
             w4_sc_raw[:].rearrange("p (a q t) -> p a t q", a=R_PASSES, t=PACK),
         )
-        resistances(0, range(3))
-        pick(0, 4)
-        quantise_w1(1, 0, 0)
-        first_product(1, 0, range(3))
-        quantise_w1(1, 1, 32)
-        quantise_w1(1, 2, VECTOR_WORDS)
-        resistances(0, [3])
-        first_product(1, 0, [3])
+        pick(0, 2)
+        quantise_w1(1, 2, nc.scalar.copy)
+        for s in (2, 3):
+            for a in range(K_PASSES):
+                first_product(s, a)
+        pick(2, 4)
+        quantise_w1(2, 0, nc.scalar.copy)
+        quantise_w1(2, 2, nc.vector.tensor_copy)
+        quantise_w1(2, 1, nc.scalar.copy)
+        resistances(2)
+        resistances(3)
+        for s in range(PACK, 2 * PACK):
+            for a in range(K_PASSES):
+                first_product(s, a)
         pick(4, 8)
-        for t in range(PACK):
-            first_product(1, 1, [t])
-            first_product(1, 2, [t])
-        resistances(1)
+        for s in range(PACK, 2 * PACK):
+            resistances(s)
         nc.scalar.copy(factor[:], inv_kap[:])
         pick(8, 12)
         for h in range(2):

@@ -25,6 +25,7 @@ BANK = 512
 HALF = J // 2
 QUARTER = J // 4
 CHUNK = 256
+LAST = R_PASSES * PACK - 1
 
 
 def tile_list_doublet_series_flow_kernel(
@@ -79,7 +80,11 @@ def tile_list_doublet_series_flow_kernel(
             (2, 2): wide_stage[:],
         }
         picked = [tile("picked%d" % i, [P, HALF], F32) for i in range(2)]
-        units = [(0, t, h) for t in range(PACK) for h in range(2)] + [(1, t, h) for h in range(2) for t in range(PACK)]
+        halves = [slice(0, HALF), slice(HALF, J)]
+        late_quarters = [slice(HALF, HALF + QUARTER), slice(HALF + QUARTER, J)]
+        units = [(s, js) for s in range(PACK) for js in halves]
+        units.extend((s, js) for js in halves for s in range(PACK, 2 * PACK))
+        units = units[:-1] + [(LAST, js) for js in late_quarters]
         total = [tile("total%d" % s, [P, J], F32) for s in range(R_PASSES * PACK)]
         z_bf = [tile("z_bf%d" % g, [P, J * PACK], BF16) for g in range(R_PASSES)]
         z_words = [tile("z_words%d" % g, [P, J], U32) for g in range(R_PASSES)]
@@ -93,7 +98,7 @@ def tile_list_doublet_series_flow_kernel(
         nc.gpsimd.memset(table_sc[:].bitcast(I32)[:, 704:], 0)
         nc.vector.memset(w4_sc_raw[:].bitcast(I32), 0)
         nc.vector.memset(v_sc[:].bitcast(I32), 0)
-        nc.vector.memset(factor[:], -1.0)
+        nc.vector.memset(factor[:, LAST : LAST + 1], -1.0)
 
         def load_w1(b, a):
             first, width = blocks[b]
@@ -174,45 +179,38 @@ def tile_list_doublet_series_flow_kernel(
                     res[s][:, h * BANK : (h + 1) * BANK],
                     banks[2 * (s % PACK) + h][:],
                     ACT.Exp,
-                    scale=factor[:, s : s + 1],
+                    scale=factor[:, s : s + 1] if s == LAST else -1.0,
                 )
 
-        def entries(h):
-            return slice(h * HALF // 16, (h + 1) * HALF // 16)
+        def entries(js):
+            return slice(js.start // 16, js.stop // 16)
 
         def landing(i):
+            width = units[i][1].stop - units[i][1].start
             if i in (0, 2):
-                return wide_stage[:].bitcast(F32)[:, :HALF]
+                return wide_stage[:].bitcast(F32)[:, :width]
             if i == 12:
-                return z_bf[0][:].bitcast(F32)[:, :HALF]
+                return z_bf[0][:].bitcast(F32)[:, :width]
             if i == 14:
-                return z_bf[0][:].bitcast(F32)[:, J : J + HALF]
+                return z_bf[0][:].bitcast(F32)[:, J : J + width]
             if i == 15:
-                return z_bf[1][:].bitcast(F32)[:, :HALF]
-            return picked[i % 2][:]
-
-        def pick_first(i):
-            g, t, h = units[i]
-            nc.vector.tensor_copy(landing(i), res[g * PACK + t][:].indirect(pos1_t[:, entries(h)]))
-
-        def pick_second(i):
-            g, t, h = units[i]
-            nc.vector.tensor_tensor(
-                total[g * PACK + t][:, h * HALF : (h + 1) * HALF], res[g * PACK + t][:].indirect(pos2_t[:, entries(h)]), landing(i), ALU.add
-            )
-            if g == 0:
-                js = slice(h * HALF, (h + 1) * HALF)
-                nc.sync.dma_start(regrouped[32 * t : 32 * (t + 1), :, js], total[t][:, js])
+                return z_bf[1][:].bitcast(F32)[:, :width]
+            return picked[i % 2][:, :width]
 
         def pick(first, last):
-            for i in range(first, last, 2):
-                pick_first(i)
-                pick_first(i + 1)
-                pick_second(i)
-                pick_second(i + 1)
+            for i in range(first, last):
+                s, js = units[i]
+                nc.vector.tensor_copy(landing(i), res[s][:].indirect(pos1_t[:, entries(js)]))
+            for i in range(first, last):
+                s, js = units[i]
+                nc.vector.tensor_tensor(
+                    total[s][:, js], res[s][:].indirect(pos2_t[:, entries(js)]), landing(i), ALU.add
+                )
+                if s < PACK:
+                    nc.sync.dma_start(regrouped[32 * s : 32 * (s + 1), :, js], total[s][:, js])
 
-        def roots(g, js):
-            for t in range(PACK):
+        def roots(g, js, slots=range(PACK)):
+            for t in slots:
                 s = g * PACK + t
                 sums_of_pairs = regrouped[:, t, js] if g == 0 else total[s][:, js]
                 nc.scalar.activation(
@@ -294,11 +292,13 @@ def tile_list_doublet_series_flow_kernel(
         for s in range(PACK, 2 * PACK):
             for a in range(K_PASSES):
                 first_product(s, a)
-        pick(4, 8)
+        pick(4, 6)
+        pick(6, 8)
         for s in range(PACK, 2 * PACK):
             resistances(s)
         nc.scalar.copy(factor[:], inv_kap[:])
-        pick(8, 12)
+        pick(8, 10)
+        pick(10, 12)
         for h in range(2):
             roots(0, slice(h * HALF, (h + 1) * HALF))
             make_z(0, slice(h * HALF, (h + 1) * HALF))
@@ -309,9 +309,11 @@ def tile_list_doublet_series_flow_kernel(
         roots(1, slice(0, HALF))
         make_z(1, slice(0, HALF))
         pick(14, 16)
-        roots(1, slice(HALF, J))
-        make_z(1, slice(HALF, HALF + QUARTER))
-        make_z(1, slice(HALF + QUARTER, J))
+        pick(16, 17)
+        roots(1, halves[1], range(PACK - 1))
+        for js in late_quarters:
+            roots(1, js, [PACK - 1])
+            make_z(1, js)
         finish(slice(0, HALF), nc.scalar.copy)
         finish(slice(HALF, HALF + QUARTER), nc.scalar.copy)
         finish(slice(HALF + QUARTER, J), nc.vector.tensor_copy)

from contextlib import ExitStack

import concourse.mybir as mybir

T, S, K, H, N, J = 4096, 1024, 1536, 1024, 512, 512
FLOPS = 2 * K * H * S + 2 * H * N * J

F32 = mybir.dt.float32
BF16 = mybir.dt.bfloat16
I32 = mybir.dt.int32
U32 = mybir.dt.uint32
U16 = mybir.dt.uint16
U8 = mybir.dt.uint8
FP8X4 = mybir.dt.float8_e4m3fn_x4
FP4X4 = mybir.dt.float4_e2m1fn_x4
ACT = mybir.ActivationFunctionType
ALU = mybir.AluOpType

P = 128
PACK = 4
PASS = P * PACK
K_PASSES = K // PASS
R_PASSES = H // PASS
BANK = 512
HALF = J // 2
QUARTER = J // 4
CHUNK = 256
LAST = R_PASSES * PACK - 1


def tile_list_doublet_series_flow_kernel(
    tc, tab_words, tab_scales, offs, pos1, pos2, w1, kap, w4_words, w4_scales, base, out_0, out_1, out_2
):
    nc = tc.nc
    with ExitStack() as ctx:
        sb = ctx.enter_context(tc.tile_pool(name="sb", bufs=1))
        ring = ctx.enter_context(tc.tile_pool(name="ring", bufs=5))
        ps = ctx.enter_context(tc.psum_pool(name="ps", bufs=1))

        def tile(name, shape, dtype):
            return sb.tile(shape, dtype, name=name, align_bytes=64)

        def load_buffer(name, shape, dtype):
            return ring.tile(shape, dtype, name=name, tag="load", align_bytes=64)

        banks = [ps.tile([P, BANK], F32, name="bank%d" % b) for b in range(8)]

        offs_t = tile("offs_t", [P, S // 16], U16)
        pos1_t = tile("pos1_t", [P, J // 16], U16)
        pos2_t = tile("pos2_t", [P, J // 16], U16)
        table = {}
        table_sc = tile("table_sc", [P, T], U8)
        v_words = [tile("v_words%d" % a, [P, S], U16) for a in range(K_PASSES)]
        picked_sc = tile("picked_sc", [P, S], U8)
        v_sc = tile("v_sc", [P, K_PASSES * S], U8)
        blocks = [(0, CHUNK), (CHUNK, CHUNK), (PASS, PASS)]
        pieces = [(b, a) for b in range(len(blocks)) for a in range(K_PASSES)]
        w1_raw = {}
        w1_words = {(b, a): tile("w1_words%d%d" % (b, a), [P, blocks[b][1]], U32) for b, a in pieces}
        w1_sc = {(b, a): tile("w1_sc%d%d" % (b, a), [P, blocks[b][1]], U8) for b, a in pieces}
        stage = [tile("stage%d" % i, [P, PACK * CHUNK], BF16) for i in range(3)]
        wide_stage = tile("wide_stage", [P, PACK * PASS], BF16)
        w4_raw = tile("w4_raw", [P, R_PASSES * N], U16)
        w4_sc_raw = tile("w4_sc_raw", [P, R_PASSES * N], U8)
        w4_dealt = tile("w4_dealt", [P, R_PASSES * N], U16)
        w4_sc = tile("w4_sc", [P, R_PASSES * N], U8)
        kap_t = tile("kap_t", [P, R_PASSES * PACK], F32)
        inv_kap = tile("inv_kap", [P, R_PASSES * PACK], F32)
        factor = tile("factor", [P, R_PASSES * PACK], F32)
        res = [tile("res%d" % s, [P, S], F32) for s in range(R_PASSES * PACK)]
        w1_bf = {
            (0, 0): stage[0][:],
            (0, 1): stage[1][:],
            (0, 2): stage[2][:],
            (1, 0): stage[0][:],
            (1, 1): stage[2][:],
            (1, 2): wide_stage[:, : PACK * CHUNK],
            (2, 0): res[2][:].bitcast(BF16),
            (2, 1): res[3][:].bitcast(BF16),
            (2, 2): wide_stage[:],
        }
        picked = [tile("picked%d" % i, [P, HALF], F32) for i in range(2)]
        halves = [slice(0, HALF), slice(HALF, J)]
        late_quarters = [slice(HALF, HALF + QUARTER), slice(HALF + QUARTER, J)]
        units = [(s, js) for s in range(PACK) for js in halves]
        units.extend((s, js) for js in halves for s in range(PACK, 2 * PACK))
        units = units[:-1] + [(LAST, js) for js in late_quarters]
        total = [tile("total%d" % s, [P, J], F32) for s in range(R_PASSES * PACK)]
        z_bf = [tile("z_bf%d" % g, [P, J * PACK], BF16) for g in range(R_PASSES)]
        z_words = [tile("z_words%d" % g, [P, J], U32) for g in range(R_PASSES)]
        z_sc = [tile("z_sc%d" % g, [P, J], U8) for g in range(R_PASSES)]
        y = tile("y", [P, PACK, J], F32)
        y_bf = tile("y_bf", [P, J * PACK], BF16)
        y_words = tile("y_words", [P, J], U32)
        y_sc = tile("y_sc", [P, J], U8)

        nc.vector.memset(table_sc[:].bitcast(I32)[:, :704], 0)
        nc.gpsimd.memset(table_sc[:].bitcast(I32)[:, 704:], 0)
        nc.vector.memset(w4_sc_raw[:].bitcast(I32), 0)
        nc.vector.memset(v_sc[:].bitcast(I32), 0)
        nc.vector.memset(factor[:, LAST : LAST + 1], -1.0)

        def load_w1(b, a):
            first, width = blocks[b]
            rows = w1[a * PASS : (a + 1) * PASS, first : first + width]
            w1_raw[b, a] = load_buffer("w1_raw%d%d" % (b, a), [P, PACK, width], F32)
            nc.sync.dma_start(w1_raw[b, a][:], rows.rearrange("(p j) c -> p j c", j=PACK))

        def load_table(a):
            table[a] = load_buffer("table%d" % a, [P, T], U16)
            nc.sync.dma_start(table[a][:].bitcast(I32), tab_words[a].bitcast(I32))

        load_table(0)
        nc.sync.dma_start(table_sc[0:96:2, :].bitcast(I32), tab_scales.bitcast(I32).rearrange("a q t -> q a t"))
        nc.sync.dma_start(offs_t[:], offs)
        nc.sync.dma_start(pos1_t[:], pos1)
        nc.vector.tensor_copy(picked_sc[:], table_sc[:].indirect(offs_t[:]))
        load_w1(0, 0)
        load_table(1)
        load_w1(0, 1)
        load_table(2)
        nc.sync.dma_start(pos2_t[:], pos2)
        for q in range(4):
            nc.sync.dma_start(
                v_sc[32 * q : 32 * q + 4, :].bitcast(I32), picked_sc[24 * q : 24 * q + 24 : 2, :].bitcast(I32)
            )
        load_w1(0, 2)
        for a in range(K_PASSES):
            load_w1(1, a)
        nc.sync.dma_start(
            w4_raw[:].bitcast(I32).rearrange("p (a c) -> p a c", a=R_PASSES),
            w4_words.bitcast(I32).rearrange("a p c -> p a c"),
        )
        for q in range(4):
            nc.sync.dma_start(
                w4_sc_raw[32 * q : 32 * q + 4, :].bitcast(I32).rearrange("r (a c) -> r a c", a=R_PASSES),
                w4_scales[:, 4 * q : 4 * q + 4, :].bitcast(I32).rearrange("a r c -> r a c"),
            )
        nc.sync.dma_start(
            kap_t[:].rearrange("p (g t) -> p g t", g=R_PASSES),
            kap.rearrange("(g p t) -> p g t", g=R_PASSES, t=PACK),
        )
        for a in range(K_PASSES):
            load_w1(2, a)
        base_t = load_buffer("base_t", [P, PACK, J], F32)
        nc.sync.dma_start(base_t[:], base.rearrange("(p t) j -> p t j", t=PACK))
        regrouped = load_buffer("regrouped", [P, PACK, J], F32)
        root = [tile("root0", [P, PACK, J], F32), regrouped]

        def quantise_w1(b, a, round_to_bf16):
            raw, bf = w1_raw[b, a][:], w1_bf[b, a]
            if b == 2:
                round_to_bf16(
                    bf.rearrange("p (t m j) -> p m j t", t=PACK, j=PACK), raw.rearrange("p j (m t) -> p m j t", t=PACK)
                )
            else:
                round_to_bf16(
                    bf.rearrange("p (c i j) -> p c j i", i=4, j=PACK), raw.rearrange("p j (c i) -> p c j i", i=4)
                )
            nc.vector.quantize_mx(w1_words[b, a][:].bitcast(FP8X4), w1_sc[b, a][:], bf)

        def first_product(s, a):
            b, u = (s // 2, s % 2) if s < PACK else (2, s - PACK)
            cols = slice(u * P, (u + 1) * P)
            for h in range(2):
                nc.tensor.matmul_mx(
                    banks[2 * (s % PACK) + h][:],
                    lhsT=w1_words[b, a][:, cols].bitcast(FP8X4),
                    lhsT_scale=w1_sc[b, a][:, cols],
                    rhs=v_words[a][:, h * BANK : (h + 1) * BANK].bitcast(FP4X4),
                    rhs_scale=v_sc[:, a * S + h * BANK : a * S + (h + 1) * BANK],
                    start=(a == 0),
                    stop=(a == K_PASSES - 1),
                )

        def resistances(s):
            for h in range(2):
                nc.scalar.activation(
                    res[s][:, h * BANK : (h + 1) * BANK],
                    banks[2 * (s % PACK) + h][:],
                    ACT.Exp,
                    scale=factor[:, s : s + 1] if s == LAST else -1.0,
                )

        def entries(js):
            return slice(js.start // 16, js.stop // 16)

        def landing(i):
            width = units[i][1].stop - units[i][1].start
            if i in (0, 2):
                return wide_stage[:].bitcast(F32)[:, :width]
            if i == 12:
                return z_bf[0][:].bitcast(F32)[:, :width]
            if i == 14:
                return z_bf[0][:].bitcast(F32)[:, J : J + width]
            if i == 15:
                return z_bf[1][:].bitcast(F32)[:, :width]
            return picked[i % 2][:, :width]

        def pick(first, last):
            for i in range(first, last):
                s, js = units[i]
                nc.vector.tensor_copy(landing(i), res[s][:].indirect(pos1_t[:, entries(js)]))
            for i in range(first, last):
                s, js = units[i]
                nc.vector.tensor_tensor(
                    total[s][:, js], res[s][:].indirect(pos2_t[:, entries(js)]), landing(i), ALU.add
                )
                if s < PACK:
                    nc.sync.dma_start(regrouped[32 * s : 32 * (s + 1), :, js], total[s][:, js])

        def roots(g, js, slots=range(PACK)):
            for t in slots:
                s = g * PACK + t
                sums_of_pairs = regrouped[:, t, js] if g == 0 else total[s][:, js]
                nc.scalar.activation(
                    root[g][:, t, js], sums_of_pairs, ACT.Abs_reciprocal_sqrt, scale=factor[:, s : s + 1]
                )

        def interleaved(bf_tile, js):
            return bf_tile[:, PACK * js.start : PACK * js.stop]

        def make_z(g, js):
            nc.scalar.activation(
                interleaved(z_bf[g], js).rearrange("p (c i t) -> p c t i", i=4, t=PACK),
                root[g][:, :, js].rearrange("p t (c i) -> p c t i", i=4),
                ACT.Square,
            )
            nc.vector.quantize_mx(z_words[g][:, js].bitcast(FP8X4), z_sc[g][:, js], interleaved(z_bf[g], js))

        def sums(quarter):
            return banks[2 * quarter][:].rearrange("p (t j) -> p t j", t=PACK)

        def second_product(g, quarter):
            js = slice(quarter * QUARTER, (quarter + 1) * QUARTER)
            for t in range(PACK):
                cols = slice(g * N + t * P, g * N + (t + 1) * P)
                nc.tensor.matmul_mx(
                    sums(quarter)[:, t, :],
                    lhsT=w4_dealt[:, cols].bitcast(FP4X4),
                    lhsT_scale=w4_sc[:, cols],
                    rhs=z_words[g][:, js].bitcast(FP8X4),
                    rhs_scale=z_sc[g][:, js],
                    start=(g == 0 and t == 0),
                    stop=(g == R_PASSES - 1 and t == PACK - 1),
                )

        def finish(js, round_y):
            for quarter in range(js.start // QUARTER, js.stop // QUARTER):
                second_product(1, quarter)
                part = slice(quarter * QUARTER, (quarter + 1) * QUARTER)
                nc.vector.tensor_tensor(y[:, :, part], sums(quarter), base_t[:, :, part], ALU.subtract)
            nc.sync.dma_start(out_0.rearrange("(p t) j -> p t j", t=PACK)[:, :, js], y[:, :, js])
            round_y(
                interleaved(y_bf, js).rearrange("p (c i t) -> p c t i", i=4, t=PACK),
                y[:, :, js].rearrange("p t (c i) -> p c t i", i=4),
            )
            nc.vector.quantize_mx(y_words[:, js].bitcast(FP8X4), y_sc[:, js], interleaved(y_bf, js))
            nc.sync.dma_start(
                out_1[0].rearrange("p m t -> p (m t)").bitcast(I32)[:, js], y_words[:, js].bitcast(I32)
            )

        for a in range(K_PASSES):
            nc.vector.tensor_copy(v_words[a][:], table[a][:].indirect(offs_t[:]))
            quantise_w1(0, a, nc.scalar.copy)
            first_product(0, a)
            first_product(1, a)
        resistances(0)
        resistances(1)
        quantise_w1(1, 0, nc.scalar.copy)
        quantise_w1(1, 1, nc.vector.tensor_copy)
        nc.vector.reciprocal(inv_kap[:], kap_t[:])
        nc.vector.tensor_copy(
            w4_dealt[:].rearrange("p (a t q) -> p a t q", a=R_PASSES, t=PACK),
            w4_raw[:].rearrange("p (a q t) -> p a t q", a=R_PASSES, t=PACK),
        )
        nc.vector.tensor_copy(
            w4_sc[:].rearrange("p (a t q) -> p a t q", a=R_PASSES, t=PACK),
            w4_sc_raw[:].rearrange("p (a q t) -> p a t q", a=R_PASSES, t=PACK),
        )
        pick(0, 2)
        quantise_w1(1, 2, nc.scalar.copy)
        for s in (2, 3):
            for a in range(K_PASSES):
                first_product(s, a)
        pick(2, 4)
        quantise_w1(2, 0, nc.scalar.copy)
        quantise_w1(2, 2, nc.vector.tensor_copy)
        quantise_w1(2, 1, nc.scalar.copy)
        resistances(2)
        resistances(3)
        for s in range(PACK, 2 * PACK):
            for a in range(K_PASSES):
                first_product(s, a)
        pick(4, 6)
        pick(6, 8)
        for s in range(PACK, 2 * PACK):
            resistances(s)
        nc.scalar.copy(factor[:], inv_kap[:])
        pick(8, 10)
        pick(10, 12)
        for h in range(2):
            roots(0, slice(h * HALF, (h + 1) * HALF))
            make_z(0, slice(h * HALF, (h + 1) * HALF))
            second_product(0, 2 * h)
            second_product(0, 2 * h + 1)
            if h == 0:
                pick(12, 14)
        roots(1, slice(0, HALF))
        make_z(1, slice(0, HALF))
        pick(14, 16)
        pick(16, 17)
        roots(1, halves[1], range(PACK - 1))
        for js in late_quarters:
            roots(1, js, [PACK - 1])
            make_z(1, js)
        finish(slice(0, HALF), nc.scalar.copy)
        finish(slice(HALF, HALF + QUARTER), nc.scalar.copy)
        finish(slice(HALF + QUARTER, J), nc.vector.tensor_copy)
        for q in range(4):
            engine = nc.sync if q % 2 == 0 else nc.scalar
            engine.dma_start(out_2[0, 4 * q : 4 * q + 4, :].bitcast(I32), y_sc[32 * q : 32 * q + 4, :].bitcast(I32))
